import numpy as np
import ml_dtypes


def mxq(x, axis, fmt="e4m3"):
    dtype, down = {"e4m3": (ml_dtypes.float8_e4m3fn, 7), "e5m2": (ml_dtypes.float8_e5m2, 14)}[fmt]
    v = np.moveaxis(np.asarray(x, np.float32).astype(ml_dtypes.bfloat16).astype(np.float64), axis, -1)
    blocks = v.reshape(v.shape[:-1] + (-1, 32))
    amax = np.abs(blocks).max(-1, keepdims=True)
    byte = np.maximum(np.where(amax > 0, np.frexp(amax)[1] - 1 + 127, 0) - down, 1)
    scale = np.exp2(byte - 127.0)
    codes = (blocks / scale).astype(np.float32).astype(dtype).astype(np.float64)
    return np.moveaxis((codes * scale).reshape(v.shape), -1, axis)


WIDE = False


def mx_kscale(k):
    if not WIDE:
        return np.ones(k)
    levels = np.array([10, -10, 5, -5, 0])
    if k % 512:
        return np.exp2(np.random.permutation(np.resize(levels, k // 32))).repeat(32)
    a = np.empty((k // 512, 16))
    for p in range(k // 512):
        a[p, :8] = np.random.permutation(np.resize(levels, 8))
        for g in range(8):
            far = levels[np.abs(levels - a[p, g]) >= 10]
            a[p, g + 8] = far[np.random.randint(len(far))]
    return np.exp2(a.ravel()).repeat(32)


def f64(x):
    return np.asarray(x).astype(np.float64)


def striped8(idx):
    return np.asarray(idx).reshape(8, -1, 16).transpose(0, 2, 1).reshape(128, -1).astype(np.uint16)


def unstriped8(offs):
    return offs.reshape(8, 16, -1).transpose(0, 2, 1).reshape(8, -1).astype(np.int64)


def pick8(x, idx, run):
    r = np.arange(len(x))
    return x[r[:, None], idx[r % (8 * run) // run]]


E2M1 = np.array([0.0, 0.5, 1.0, 1.5, 2.0, 3.0, 4.0, 6.0, -0.0, -0.5, -1.0, -1.5, -2.0, -3.0, -4.0, -6.0])


def pack_weight(w, fmt):
    k, n = w.shape
    w = f64(np.asarray(w, np.float32).astype(ml_dtypes.bfloat16)).reshape(k // 32, 32, n)
    amax = np.abs(w).max(1)
    if fmt == "e4m3":
        byte = np.frexp(amax)[1] - 1 + 127 - 7
    else:
        mant, ex = np.frexp(amax / 6.0)
        byte = np.where(mant > 0.5, ex, ex - 1) + 127
    byte = np.clip(np.where(amax > 0, byte, 1), 1, 254)
    scaled = (w * np.exp2(127.0 - byte)[:, None, :]).reshape(k, n).astype(np.float32)
    by_word = np.ascontiguousarray(scaled.reshape(k // 512, 128, 4, n).transpose(0, 1, 3, 2))
    if fmt == "e4m3":
        words = by_word.astype(ml_dtypes.float8_e4m3fn).view(np.uint8)
    else:
        c = by_word.astype(ml_dtypes.float4_e2m1fn).view(np.uint8) & 0xF
        words = (c[..., 0::2] | (c[..., 1::2] << 4)).reshape(k // 512, 128, 2 * n)
    return np.ascontiguousarray(words), np.ascontiguousarray(byte.astype(np.uint8).reshape(k // 512, 16, n))


def unpack_weight(words, scales, fmt):
    g, _, n = scales.shape
    words = np.ascontiguousarray(words).reshape(g, 128, n, -1)
    if fmt == "e4m3":
        vals = words.view(ml_dtypes.float8_e4m3fn).astype(np.float64)
    else:
        nib = np.empty((g, 128, n, 4), np.uint8)
        nib[..., 0::2] = words & 0xF
        nib[..., 1::2] = words >> 4
        vals = E2M1[nib]
    vals = vals * np.repeat(np.exp2(scales.astype(np.float64) - 127.0), 8, axis=1)[..., None]
    return vals.transpose(0, 1, 3, 2).reshape(g * 512, n)


D, T, U, I, Q, E = 512, 1024, 1024, 512, 512, 256


def setup_inputs():
    n = np.random.standard_normal
    idx = np.stack([np.random.permutation(T)[:I] for _ in range(8)])
    idx2 = np.stack([np.random.permutation(U)[:I] for _ in range(8)])
    idx3 = np.stack([np.random.permutation(U)[:I] for _ in range(8)])
    idx4 = np.stack([np.random.permutation(U)[:I] for _ in range(8)])
    idx5 = np.stack([np.random.permutation(T)[:I] for _ in range(8)])
    idx6 = np.stack([np.random.permutation(T)[:I] for _ in range(8)])
    fd = mx_kscale(D)
    fq = mx_kscale(Q)
    keysp = pack_weight(n((D, T)) / fd[:, None], "e2m1")
    notesp = pack_weight(n((D, U)) / fd[:, None], "e4m3")
    mixp = pack_weight(n((Q, E)) * 1.0 / np.sqrt(Q) / fq[:, None], "e4m3")
    return {
        "query": (n((D, Q)) * 1.0 / np.sqrt(D) * fd[:, None]).astype(np.float32),
        "query2": (n((D, Q)) * 1.0 / np.sqrt(D) * fd[:, None]).astype(np.float32),
        "keys_words": keysp[0],
        "keys_scales": keysp[1],
        "notes_words": notesp[0],
        "notes_scales": notesp[1],
        "rowf": (np.random.uniform(0.5, 2.0, (Q, 1)) * fq[:, None]).astype(np.float32),
        "mix_words": mixp[0],
        "mix_scales": mixp[1],
        "offs": striped8(idx),
        "offs2": striped8(idx2),
        "offs3": striped8(idx3),
        "offs4": striped8(idx4),
        "offs5": striped8(idx5),
        "offs6": striped8(idx6),
    }


def reference(query, query2, keys_words, keys_scales, notes_words, notes_scales, rowf, mix_words, mix_scales, offs, offs2, offs3, offs4, offs5, offs6):
    idx = unstriped8(offs)
    idx2 = unstriped8(offs2)
    idx3 = unstriped8(offs3)
    idx4 = unstriped8(offs4)
    idx5 = unstriped8(offs5)
    idx6 = unstriped8(offs6)
    keysu = unpack_weight(keys_words, keys_scales, "e2m1")
    notesu = unpack_weight(notes_words, notes_scales, "e4m3")
    mixu = unpack_weight(mix_words, mix_scales, "e4m3")
    queryq = mxq(f64(query), 0, "e4m3")
    a = queryq.T @ keysu
    query2q = mxq(f64(query2), 0, "e4m3")
    b = query2q.T @ notesu
    f1 = np.zeros((Q, U))
    f1[np.arange(Q)[:, None], idx2[np.arange(Q) % 512 // 64]] = pick8(a, idx, 64)
    w = np.maximum(pick8(f1, idx3, 64), pick8(b, idx4, 64))
    f2 = np.zeros((Q, T))
    f2[np.arange(Q)[:, None], idx5[np.arange(Q) % 512 // 64]] = w
    cc = a + f2
    g = pick8(cc, idx6, 64)
    gw = g * f64(rowf)
    gwq = mxq(gw, 0, "e4m3")
    y = mixu.T @ gwq
    return y

@@ -1,0 +1,197 @@
+from contextlib import ExitStack
+
+import concourse.mybir as mybir
+
+D, T, U, I, Q, E = 512, 1024, 1024, 512, 512, 256
+FLOPS = 2 * D * Q * T + 2 * D * Q * U + 2 * Q * E * I
+
+F32 = mybir.dt.float32
+BF16 = mybir.dt.bfloat16
+I32 = mybir.dt.int32
+U32 = mybir.dt.uint32
+U16 = mybir.dt.uint16
+U8 = mybir.dt.uint8
+FP8X4 = mybir.dt.float8_e4m3fn_x4
+FP4X4 = mybir.dt.float4_e2m1fn_x4
+COPY = mybir.ActivationFunctionType.Copy
+ALU = mybir.AluOpType
+
+P = 128
+PACK = 4
+BANK = 512
+HALF = I // 2
+
+
+def tile_attend_returned_twoq_mixed_kernel(tc, query, query2, keys_words, keys_scales, notes_words, notes_scales,
+                                            rowf, mix_words, mix_scales, offs, offs2, offs3, offs4, offs5, offs6, out):
+    nc = tc.nc
+    with ExitStack() as ctx:
+        keep = ctx.enter_context(tc.tile_pool(name="keep", bufs=1))
+        ring = ctx.enter_context(tc.tile_pool(name="ring", bufs=2))
+        pairs = ctx.enter_context(tc.tile_pool(name="pairs", bufs=1))
+        score_banks = ctx.enter_context(tc.psum_pool(name="score_banks", bufs=6))
+        out_banks = ctx.enter_context(tc.psum_pool(name="out_banks", bufs=1))
+
+        def load_list(source, name):
+            tile = keep.tile([P, I // 16], U16, name=name)
+            nc.sync.dma_start(tile[:], source)
+            return tile
+
+        def zeroed_plane(width, name):
+            plane = keep.tile([P, width], U8, name=name, align_bytes=64)
+            nc.vector.memset(plane[:].bitcast(U32), 0)
+            return plane
+
+        def load_plane(queue, plane, scales):
+            for quad in range(4):
+                queue.dma_start(out=plane[32 * quad:32 * quad + 4, :].bitcast(I32),
+                                in_=scales[0, 4 * quad:4 * quad + 4, :].bitcast(I32))
+
+        def load_query(source, name, parts):
+            rows = source.rearrange("(p j) q -> p j q", j=PACK)
+            width = Q // parts
+            raws = []
+            for h in range(parts):
+                raw = keep.tile([P, PACK, width], F32, name="%s_raw%d" % (name, h))
+                nc.sync.dma_start(out=raw[:], in_=rows[:, :, h * width:(h + 1) * width])
+                raws.append(raw)
+            return raws
+
+        def deal_query(raws, name, cast):
+            dealt = keep.tile([P, PACK, P, PACK], BF16, name=name + "_dealt", align_bytes=64)
+            width = P // len(raws)
+            for h, raw in enumerate(raws):
+                cast(out=dealt[:, :, h * width:(h + 1) * width, :].rearrange("p t m j -> p m j t"),
+                     in_=raw[:].rearrange("p j (m t) -> p m j t", t=PACK))
+            return dealt
+
+        def quantize_tiles(dealt, first, count, name):
+            codes = keep.tile([P, count * P], U32, name=name + "_codes", align_bytes=64)
+            scales = keep.tile([P, count * P], U8, name=name + "_scales", align_bytes=64)
+            nc.vector.quantize_mx(out=codes[:].bitcast(FP8X4), scales=scales[:],
+                                  in_=dealt[:, first:first + count].rearrange("p t m j -> p (t m j)"))
+            return [(codes[:, k * P:(k + 1) * P].bitcast(FP8X4), scales[:, k * P:(k + 1) * P]) for k in range(count)]
+
+        def score(rows, moving, plane, name, engines):
+            scores = keep.tile([P, 2 * BANK], F32, name=name)
+            for n in range(2):
+                bank = score_banks.tile([P, BANK], F32, name="bank")
+                nc.tensor.matmul_mx(out=bank[:], lhsT=rows[0], lhsT_scale=rows[1], rhs=moving[n],
+                                    rhs_scale=plane[:, n * BANK:(n + 1) * BANK], start=True, stop=True)
+                engines[n](out=scores[:, n * BANK:(n + 1) * BANK], in_=bank[:])
+            return scores
+
+        def gather(picked, window, offsets):
+            nc.scalar.activation(picked, window[:].indirect(offsets), COPY)
+
+        keys_plane = zeroed_plane(T, "keys_plane")
+        notes_plane = zeroed_plane(U, "notes_plane")
+        mix_plane = zeroed_plane(E, "mix_plane")
+        f1 = [keep.tile([P, U], F32, name="f1_%d" % k) for k in range(2)]
+        f2 = [keep.tile([P, T], F32, name="f2_%d" % k) for k in range(2)]
+        for tile in f1 + f2:
+            nc.vector.memset(tile[:], 0.0)
+
+        load_plane(nc.scalar, keys_plane, keys_scales)
+        query_raw = load_query(query, "query", 2)
+        keys_codes = keep.tile([P, 2 * T], U8, name="keys_codes", align_bytes=64)
+        nc.sync.dma_start(out=keys_codes[:].bitcast(I32), in_=keys_words[0].bitcast(I32))
+        list1 = load_list(offs, "list1")
+        list2 = load_list(offs2, "list2")
+        query2_raw = load_query(query2, "query2", 1)
+        notes_codes = keep.tile([P, U], U32, name="notes_codes", align_bytes=64)
+        nc.sync.dma_start(out=notes_codes[:].bitcast(I32),
+                          in_=notes_words[0].rearrange("p n r -> p (n r)").bitcast(I32))
+        load_plane(nc.sync, notes_plane, notes_scales)
+        list3 = load_list(offs3, "list3")
+        list4 = load_list(offs4, "list4")
+        list5 = load_list(offs5, "list5")
+        list6 = load_list(offs6, "list6")
+        factors = keep.tile([P, PACK], F32, name="factors")
+        nc.sync.dma_start(out=factors[:], in_=rowf.rearrange("(p t) o -> p (t o)", t=PACK))
+        mix_codes = keep.tile([P, E], U32, name="mix_codes", align_bytes=64)
+        nc.sync.dma_start(out=mix_codes[:].bitcast(I32),
+                          in_=mix_words[0].rearrange("p n r -> p (n r)").bitcast(I32))
+        load_plane(nc.sync, mix_plane, mix_scales)
+
+        keys_moving = [keys_codes[:, 2 * n * BANK:2 * (n + 1) * BANK].bitcast(FP4X4) for n in range(2)]
+        notes_moving = [notes_codes[:, n * BANK:(n + 1) * BANK].bitcast(FP8X4) for n in range(2)]
+        both_scalar = (nc.scalar.copy, nc.scalar.copy)
+
+        dealt = deal_query(query_raw, "query", nc.vector.tensor_copy)
+        rows = quantize_tiles(dealt, 0, 1, "q0") + quantize_tiles(dealt, 1, 1, "q1") + quantize_tiles(dealt, 2, 2, "q2")
+
+        halves = [slice(h * HALF, (h + 1) * HALF) for h in range(2)]
+        list_halves = [slice(h * HALF // 16, (h + 1) * HALF // 16) for h in range(2)]
+        f1_picked = [pairs.tile([P, 2, I], F32, name="f1_picked%d" % k, tag="pair%d" % k) for k in range(2)]
+        b_picked = [keep.tile([P, 2, I], F32, name="b_picked%d" % k) for k in range(2)]
+
+        a, rows2 = [], []
+        for t in range(PACK):
+            engines = (nc.scalar.copy, nc.vector.tensor_copy) if t == 0 else both_scalar
+            a.append(score(rows[t], keys_moving, keys_plane, "a%d" % t, engines))
+            if t == 0:
+                for h in range(2):
+                    a_half = keep.tile([P, HALF], F32, name="a_half%d" % h)
+                    gather(a_half[:], a[t], list1[:, list_halves[h]])
+                    nc.vector.tensor_copy(f1[0][:].indirect(list2[:, list_halves[h]]), a_half[:])
+                rows2 = quantize_tiles(deal_query(query2_raw, "query2", nc.vector.tensor_copy), 0, PACK, "q2all")
+            else:
+                a_picked = ring.tile([P, I], F32, name="a_picked")
+                gather(a_picked[:], a[t], list1[:])
+                if t >= 2:
+                    gather(f1_picked[0][:, t % 2, :], f1[t % 2], list3[:])
+                nc.vector.tensor_copy(f1[t % 2][:].indirect(list2[:]), a_picked[:])
+
+        for t in range(PACK):
+            if t >= 2:
+                gather(f1_picked[1][:, t % 2, :], f1[t % 2], list3[:])
+            b = score(rows2[t], notes_moving, notes_plane, "b%d" % t, both_scalar)
+            gather(b_picked[t // 2][:, t % 2, :], b, list4[:])
+
+        gw = keep.tile([P, I, PACK], BF16, name="gw", align_bytes=64)
+        g_last = []
+
+        def finish(t, cc, add):
+            add(cc[:], a[t][:], f2[t % 2][:], ALU.add)
+            g = keep.tile([P, I], F32, name="g%d" % t, tag="g%d" % min(t, PACK - 2))
+            if t < PACK - 1:
+                gather(g[:], cc, list6[:])
+                nc.scalar.activation(gw[:, :, t], g[:], COPY, scale=factors[:, t:t + 1])
+            else:
+                for h in range(2):
+                    gather(g[:, halves[h]], cc, list6[:, list_halves[h]])
+                    g_last.append(g[:, halves[h]])
+
+        def larger(k):
+            w = keep.tile([P, 2, I], F32, name="w%d" % k)
+            nc.vector.tensor_tensor(w[:], f1_picked[k][:], b_picked[k][:], ALU.max)
+            return w
+
+        w = larger(0)
+        for t in range(2):
+            nc.vector.tensor_copy(f2[t][:].indirect(list5[:]), w[:, t, :])
+        finish(0, pairs.tile([P, T], F32, name="cc0", tag="pair0"), nc.vector.tensor_tensor)
+        w = larger(1)
+        finish(1, pairs.tile([P, T], F32, name="cc1", tag="pair1"), nc.vector.tensor_tensor)
+        for t in range(2):
+            nc.vector.tensor_copy(f2[t][:].indirect(list5[:]), w[:, t, :])
+        finish(2, keep.tile([P, T], F32, name="cc2"), nc.vector.tensor_tensor)
+        finish(3, keep.tile([P, T], F32, name="cc3"), nc.vector.tensor_tensor)
+
+        out_view = out.rearrange("(c p) i -> p c i", p=P)
+        for h in range(2):
+            slots = halves[h]
+            nc.vector.tensor_scalar(gw[:, slots, PACK - 1], g_last[h], factors[:, PACK - 1:PACK], None, ALU.mult)
+            gw_codes = keep.tile([P, HALF], U32, name="gw_codes%d" % h, align_bytes=64)
+            gw_scales = keep.tile([P, HALF], U8, name="gw_scales%d" % h, align_bytes=64)
+            nc.vector.quantize_mx(out=gw_codes[:].bitcast(FP8X4), scales=gw_scales[:],
+                                  in_=gw[:, slots, :].rearrange("p i t -> p (i t)"))
+            bank = out_banks.tile([P, E // P, HALF], F32, name="out_bank%d" % h)
+            for c in range(E // P):
+                nc.tensor.matmul_mx(out=bank[:, c, :], lhsT=mix_codes[:, c * P:(c + 1) * P].bitcast(FP8X4),
+                                    lhsT_scale=mix_plane[:, c * P:(c + 1) * P], rhs=gw_codes[:].bitcast(FP8X4),
+                                    rhs_scale=gw_scales[:], start=True, stop=True)
+            result = keep.tile([P, E // P, HALF], F32, name="result%d" % h)
+            nc.scalar.copy(out=result[:], in_=bank[:])
+            nc.sync.dma_start(out=out_view[:, :, slots], in_=result[:])

@@ -28,9 +28,7 @@ def tile_attend_returned_twoq_mixed_kernel(tc, query, query2, keys_words, keys_s
     with ExitStack() as ctx:
         keep = ctx.enter_context(tc.tile_pool(name="keep", bufs=1))
         ring = ctx.enter_context(tc.tile_pool(name="ring", bufs=2))
-        pairs = ctx.enter_context(tc.tile_pool(name="pairs", bufs=1))
-        score_banks = ctx.enter_context(tc.psum_pool(name="score_banks", bufs=6))
-        out_banks = ctx.enter_context(tc.psum_pool(name="out_banks", bufs=1))
+        score_banks = ctx.enter_context(tc.psum_pool(name="score_banks", bufs=8))
 
         def load_list(source, name):
             tile = keep.tile([P, I // 16], U16, name=name)
@@ -42,28 +40,22 @@ def tile_attend_returned_twoq_mixed_kernel(tc, query, query2, keys_words, keys_s
             nc.vector.memset(plane[:].bitcast(U32), 0)
             return plane
 
-        def load_plane(queue, plane, scales):
+        def load_plane(plane, scales):
             for quad in range(4):
-                queue.dma_start(out=plane[32 * quad:32 * quad + 4, :].bitcast(I32),
+                nc.sync.dma_start(out=plane[32 * quad:32 * quad + 4, :].bitcast(I32),
                                 in_=scales[0, 4 * quad:4 * quad + 4, :].bitcast(I32))
 
-        def load_query(source, name, parts):
-            rows = source.rearrange("(p j) q -> p j q", j=PACK)
-            width = Q // parts
-            raws = []
-            for h in range(parts):
-                raw = keep.tile([P, PACK, width], F32, name="%s_raw%d" % (name, h))
-                nc.sync.dma_start(out=raw[:], in_=rows[:, :, h * width:(h + 1) * width])
-                raws.append(raw)
-            return raws
+        def load_query(source, name, first, end):
+            raw = keep.tile([P, PACK, end - first], F32, name=name)
+            nc.sync.dma_start(out=raw[:], in_=source.rearrange("(p j) q -> p j q", j=PACK)[:, :, first:end])
+            return raw
 
-        def deal_query(raws, name, cast):
-            dealt = keep.tile([P, PACK, P, PACK], BF16, name=name + "_dealt", align_bytes=64)
-            width = P // len(raws)
-            for h, raw in enumerate(raws):
-                cast(out=dealt[:, :, h * width:(h + 1) * width, :].rearrange("p t m j -> p m j t"),
-                     in_=raw[:].rearrange("p j (m t) -> p m j t", t=PACK))
-            return dealt
+        def deal(cast, dealt, raw, rows, tiles, walk):
+            cast(out=dealt[:, tiles, rows, :].rearrange("p t m j -> " + walk),
+                 in_=raw[:].rearrange("p j (m t) -> p t m j", t=PACK)[:, tiles].rearrange("p t m j -> " + walk))
+
+        def gpsimd_round(out, in_):
+            nc.gpsimd.tensor_scalar(out, in_, 1.0, 0.0, ALU.mult, ALU.add)
 
         def quantize_tiles(dealt, first, count, name):
             codes = keep.tile([P, count * P], U32, name=name + "_codes", align_bytes=64)
@@ -73,12 +65,14 @@ def tile_attend_returned_twoq_mixed_kernel(tc, query, query2, keys_words, keys_s
             return [(codes[:, k * P:(k + 1) * P].bitcast(FP8X4), scales[:, k * P:(k + 1) * P]) for k in range(count)]
 
         def score(rows, moving, plane, name, engines):
-            scores = keep.tile([P, 2 * BANK], F32, name=name)
-            for n in range(2):
+            scores = keep.tile([P, T], F32, name=name, tag=name)
+            width = T // len(engines)
+            for n, copy_out in enumerate(engines):
+                cols = slice(n * width, (n + 1) * width)
                 bank = score_banks.tile([P, BANK], F32, name="bank")
-                nc.tensor.matmul_mx(out=bank[:], lhsT=rows[0], lhsT_scale=rows[1], rhs=moving[n],
-                                    rhs_scale=plane[:, n * BANK:(n + 1) * BANK], start=True, stop=True)
-                engines[n](out=scores[:, n * BANK:(n + 1) * BANK], in_=bank[:])
+                nc.tensor.matmul_mx(out=bank[:, :width], lhsT=rows[0], lhsT_scale=rows[1], rhs=moving(cols),
+                                    rhs_scale=plane[:, cols], start=True, stop=True)
+                copy_out(out=scores[:, cols], in_=bank[:, :width])
             return scores
 
         def gather(picked, window, offsets):
@@ -87,22 +81,25 @@ def tile_attend_returned_twoq_mixed_kernel(tc, query, query2, keys_words, keys_s
         keys_plane = zeroed_plane(T, "keys_plane")
         notes_plane = zeroed_plane(U, "notes_plane")
         mix_plane = zeroed_plane(E, "mix_plane")
-        f1 = [keep.tile([P, U], F32, name="f1_%d" % k) for k in range(2)]
+        f1 = [keep.tile([P, U], F32, name="f1_%d" % k) for k in range(PACK - 1)]
         f2 = [keep.tile([P, T], F32, name="f2_%d" % k) for k in range(2)]
-        for tile in f1 + f2:
+        for tile in f1:
             nc.vector.memset(tile[:], 0.0)
+        for tile in f2:
+            nc.gpsimd.memset(tile[:], 0.0)
 
-        load_plane(nc.scalar, keys_plane, keys_scales)
-        query_raw = load_query(query, "query", 2)
+        query_raw = [load_query(query, "query_raw0", 0, Q // 2)]
+        load_plane(keys_plane, keys_scales)
+        query_raw.append(load_query(query, "query_raw1", Q // 2, Q))
         keys_codes = keep.tile([P, 2 * T], U8, name="keys_codes", align_bytes=64)
         nc.sync.dma_start(out=keys_codes[:].bitcast(I32), in_=keys_words[0].bitcast(I32))
         list1 = load_list(offs, "list1")
         list2 = load_list(offs2, "list2")
-        query2_raw = load_query(query2, "query2", 1)
+        query2_raw = load_query(query2, "query2_raw", 0, Q)
         notes_codes = keep.tile([P, U], U32, name="notes_codes", align_bytes=64)
         nc.sync.dma_start(out=notes_codes[:].bitcast(I32),
                           in_=notes_words[0].rearrange("p n r -> p (n r)").bitcast(I32))
-        load_plane(nc.sync, notes_plane, notes_scales)
+        load_plane(notes_plane, notes_scales)
         list3 = load_list(offs3, "list3")
         list4 = load_list(offs4, "list4")
         list5 = load_list(offs5, "list5")
@@ -112,74 +109,89 @@ def tile_attend_returned_twoq_mixed_kernel(tc, query, query2, keys_words, keys_s
         mix_codes = keep.tile([P, E], U32, name="mix_codes", align_bytes=64)
         nc.sync.dma_start(out=mix_codes[:].bitcast(I32),
                           in_=mix_words[0].rearrange("p n r -> p (n r)").bitcast(I32))
-        load_plane(nc.sync, mix_plane, mix_scales)
+        load_plane(mix_plane, mix_scales)
 
-        keys_moving = [keys_codes[:, 2 * n * BANK:2 * (n + 1) * BANK].bitcast(FP4X4) for n in range(2)]
-        notes_moving = [notes_codes[:, n * BANK:(n + 1) * BANK].bitcast(FP8X4) for n in range(2)]
+        def keys_moving(cols):
+            return keys_codes[:, 2 * cols.start:2 * cols.stop].bitcast(FP4X4)
+
+        def notes_moving(cols):
+            return notes_codes[:, cols].bitcast(FP8X4)
+
         both_scalar = (nc.scalar.copy, nc.scalar.copy)
+        in_turn = (nc.scalar.copy, nc.vector.tensor_copy) * 2
 
-        dealt = deal_query(query_raw, "query", nc.vector.tensor_copy)
-        rows = quantize_tiles(dealt, 0, 1, "q0") + quantize_tiles(dealt, 1, 1, "q1") + quantize_tiles(dealt, 2, 2, "q2")
+        dealt = keep.tile([P, PACK, P, PACK], BF16, name="dealt", align_bytes=64)
+        deal(nc.vector.tensor_copy, dealt, query_raw[0], slice(0, P // 2), slice(0, PACK), "p m j t")
+        deal(nc.vector.tensor_copy, dealt, query_raw[1], slice(P // 2, P), slice(0, 1), "p m j t")
+        rows = quantize_tiles(dealt, 0, 1, "q0")
+        deal(nc.vector.tensor_copy, dealt, query_raw[1], slice(P // 2, P), slice(1, PACK), "p m j t")
+        rows = rows + quantize_tiles(dealt, 1, 1, "q1") + quantize_tiles(dealt, 2, 2, "q2")
 
         halves = [slice(h * HALF, (h + 1) * HALF) for h in range(2)]
         list_halves = [slice(h * HALF // 16, (h + 1) * HALF // 16) for h in range(2)]
-        f1_picked = [pairs.tile([P, 2, I], F32, name="f1_picked%d" % k, tag="pair%d" % k) for k in range(2)]
-        b_picked = [keep.tile([P, 2, I], F32, name="b_picked%d" % k) for k in range(2)]
 
-        a, rows2 = [], []
+        a, rows2, f1_picked = [], [], []
         for t in range(PACK):
-            engines = (nc.scalar.copy, nc.vector.tensor_copy) if t == 0 else both_scalar
-            a.append(score(rows[t], keys_moving, keys_plane, "a%d" % t, engines))
+            a.append(score(rows[t], keys_moving, keys_plane, "a%d" % t, in_turn if t == 0 else both_scalar))
             if t == 0:
                 for h in range(2):
                     a_half = keep.tile([P, HALF], F32, name="a_half%d" % h)
-                    gather(a_half[:], a[t], list1[:, list_halves[h]])
+                    if h == 0:
+                        nc.vector.tensor_copy(a_half[:], a[t][:].indirect(list1[:, list_halves[h]]))
+                    else:
+                        gather(a_half[:], a[t], list1[:, list_halves[h]])
                     nc.vector.tensor_copy(f1[0][:].indirect(list2[:, list_halves[h]]), a_half[:])
-                rows2 = quantize_tiles(deal_query(query2_raw, "query2", nc.vector.tensor_copy), 0, PACK, "q2all")
+                dealt2 = keep.tile([P, PACK, P, PACK], BF16, name="dealt2", tag="dealt2", align_bytes=64)
+                deal(gpsimd_round, dealt2, query2_raw, slice(0, P), slice(0, PACK), "p t m j")
+                rows2 = quantize_tiles(dealt2, 0, PACK, "q2all")
+                f1.append(keep.tile([P, U], F32, name="f1_3", tag="dealt2", align_bytes=64))
+                nc.gpsimd.memset(f1[PACK - 1][:], 0.0)
             else:
                 a_picked = ring.tile([P, I], F32, name="a_picked")
                 gather(a_picked[:], a[t], list1[:])
-                if t >= 2:
-                    gather(f1_picked[0][:, t % 2, :], f1[t % 2], list3[:])
-                nc.vector.tensor_copy(f1[t % 2][:].indirect(list2[:]), a_picked[:])
+                if t == PACK - 1:
+                    f1_picked.append(keep.tile([P, I], F32, name="f1_picked0"))
+                    gather(f1_picked[0][:], f1[0], list3[:])
+                nc.vector.tensor_copy(f1[t][:].indirect(list2[:]), a_picked[:])
 
+        b_picked = []
         for t in range(PACK):
-            if t >= 2:
-                gather(f1_picked[1][:, t % 2, :], f1[t % 2], list3[:])
+            if t > 0:
+                f1_picked.append(keep.tile([P, I], F32, name="f1_picked%d" % t, tag="b%d" % (t - 1)))
+                gather(f1_picked[t][:], f1[t], list3[:])
             b = score(rows2[t], notes_moving, notes_plane, "b%d" % t, both_scalar)
-            gather(b_picked[t // 2][:, t % 2, :], b, list4[:])
+            b_picked.append(keep.tile([P, I], F32, name="b_picked%d" % t))
+            gather(b_picked[t][:], b, list4[:])
 
         gw = keep.tile([P, I, PACK], BF16, name="gw", align_bytes=64)
         g_last = []
 
-        def finish(t, cc, add):
+        def larger(t):
+            w = ring.tile([P, I], F32, name="w")
+            nc.vector.tensor_tensor(w[:], f1_picked[t][:], b_picked[t][:], ALU.max)
+            return w
+
+        w = larger(0)
+        for t in range(PACK):
+            nc.vector.tensor_copy(f2[t % 2][:].indirect(list5[:]), w[:])
+            last = t == PACK - 1
+            if not last:
+                w = larger(t + 1)
+            cc = keep.tile([P, T], F32, name="cc%d" % t, tag="cc3" if last else "b%d" % t)
+            add = nc.vector.tensor_tensor if last else nc.gpsimd.tensor_tensor
             add(cc[:], a[t][:], f2[t % 2][:], ALU.add)
-            g = keep.tile([P, I], F32, name="g%d" % t, tag="g%d" % min(t, PACK - 2))
-            if t < PACK - 1:
+            g = keep.tile([P, I], F32, name="g%d" % t, tag="b3" if t == 0 else "g%d" % t)
+            if not last:
                 gather(g[:], cc, list6[:])
-                nc.scalar.activation(gw[:, :, t], g[:], COPY, scale=factors[:, t:t + 1])
+                if t < 2:
+                    nc.scalar.activation(gw[:, :, t], g[:], COPY, scale=factors[:, t:t + 1])
+                else:
+                    nc.vector.tensor_scalar(gw[:, :, t], g[:], factors[:, t:t + 1], None, ALU.mult)
             else:
                 for h in range(2):
                     gather(g[:, halves[h]], cc, list6[:, list_halves[h]])
                     g_last.append(g[:, halves[h]])
 
-        def larger(k):
-            w = keep.tile([P, 2, I], F32, name="w%d" % k)
-            nc.vector.tensor_tensor(w[:], f1_picked[k][:], b_picked[k][:], ALU.max)
-            return w
-
-        w = larger(0)
-        for t in range(2):
-            nc.vector.tensor_copy(f2[t][:].indirect(list5[:]), w[:, t, :])
-        finish(0, pairs.tile([P, T], F32, name="cc0", tag="pair0"), nc.vector.tensor_tensor)
-        w = larger(1)
-        finish(1, pairs.tile([P, T], F32, name="cc1", tag="pair1"), nc.vector.tensor_tensor)
-        for t in range(2):
-            nc.vector.tensor_copy(f2[t][:].indirect(list5[:]), w[:, t, :])
-        finish(2, keep.tile([P, T], F32, name="cc2"), nc.vector.tensor_tensor)
-        finish(3, keep.tile([P, T], F32, name="cc3"), nc.vector.tensor_tensor)
-
-        out_view = out.rearrange("(c p) i -> p c i", p=P)
         for h in range(2):
             slots = halves[h]
             nc.vector.tensor_scalar(gw[:, slots, PACK - 1], g_last[h], factors[:, PACK - 1:PACK], None, ALU.mult)
@@ -187,11 +199,12 @@ def tile_attend_returned_twoq_mixed_kernel(tc, query, query2, keys_words, keys_s
             gw_scales = keep.tile([P, HALF], U8, name="gw_scales%d" % h, align_bytes=64)
             nc.vector.quantize_mx(out=gw_codes[:].bitcast(FP8X4), scales=gw_scales[:],
                                   in_=gw[:, slots, :].rearrange("p i t -> p (i t)"))
-            bank = out_banks.tile([P, E // P, HALF], F32, name="out_bank%d" % h)
             for c in range(E // P):
-                nc.tensor.matmul_mx(out=bank[:, c, :], lhsT=mix_codes[:, c * P:(c + 1) * P].bitcast(FP8X4),
+                bank = score_banks.tile([P, BANK], F32, name="bank")
+                nc.tensor.matmul_mx(out=bank[:, :HALF], lhsT=mix_codes[:, c * P:(c + 1) * P].bitcast(FP8X4),
                                     lhsT_scale=mix_plane[:, c * P:(c + 1) * P], rhs=gw_codes[:].bitcast(FP8X4),
                                     rhs_scale=gw_scales[:], start=True, stop=True)
-            result = keep.tile([P, E // P, HALF], F32, name="result%d" % h)
-            nc.scalar.copy(out=result[:], in_=bank[:])
-            nc.sync.dma_start(out=out_view[:, :, slots], in_=result[:])
+                result = keep.tile([P, HALF], F32, name="result%d_%d" % (h, c))
+                copy_out = nc.vector.tensor_copy if (h, c) == (1, 1) else nc.scalar.copy
+                copy_out(out=result[:], in_=bank[:, :HALF])
+                nc.sync.dma_start(out=out[c * P:(c + 1) * P, slots], in_=result[:])

@@ -35,14 +35,13 @@ def tile_attend_returned_twoq_mixed_kernel(tc, query, query2, keys_words, keys_s
             nc.sync.dma_start(tile[:], source)
             return tile
 
-        def zeroed_plane(width, name):
+        def scale_plane(width, name):
             plane = keep.tile([P, width], U8, name=name, align_bytes=64)
-            nc.vector.memset(plane[:].bitcast(U32), 0)
             return plane
 
-        def load_plane(plane, scales):
+        def load_plane(queue, plane, scales):
             for quad in range(4):
-                nc.sync.dma_start(out=plane[32 * quad:32 * quad + 4, :].bitcast(I32),
+                queue.dma_start(out=plane[32 * quad:32 * quad + 4, :].bitcast(I32),
                                 in_=scales[0, 4 * quad:4 * quad + 4, :].bitcast(I32))
 
         def load_query(source, name, first, end):
@@ -57,8 +56,8 @@ def tile_attend_returned_twoq_mixed_kernel(tc, query, query2, keys_words, keys_s
         def gpsimd_round(out, in_):
             nc.gpsimd.tensor_scalar(out, in_, 1.0, 0.0, ALU.mult, ALU.add)
 
-        def quantize_tiles(dealt, first, count, name):
-            codes = keep.tile([P, count * P], U32, name=name + "_codes", align_bytes=64)
+        def quantize_tiles(dealt, first, count, name, tag=None):
+            codes = keep.tile([P, count * P], U32, name=name + "_codes", tag=tag or name + "_codes", align_bytes=64)
             scales = keep.tile([P, count * P], U8, name=name + "_scales", align_bytes=64)
             nc.vector.quantize_mx(out=codes[:].bitcast(FP8X4), scales=scales[:],
                                   in_=dealt[:, first:first + count].rearrange("p t m j -> p (t m j)"))
@@ -78,18 +77,15 @@ def tile_attend_returned_twoq_mixed_kernel(tc, query, query2, keys_words, keys_s
         def gather(picked, window, offsets):
             nc.scalar.activation(picked, window[:].indirect(offsets), COPY)
 
-        keys_plane = zeroed_plane(T, "keys_plane")
-        notes_plane = zeroed_plane(U, "notes_plane")
-        mix_plane = zeroed_plane(E, "mix_plane")
+        keys_plane = scale_plane(T, "keys_plane")
+        notes_plane = scale_plane(U, "notes_plane")
+        mix_plane = scale_plane(E, "mix_plane")
         f1 = [keep.tile([P, U], F32, name="f1_%d" % k) for k in range(PACK - 1)]
-        f2 = [keep.tile([P, T], F32, name="f2_%d" % k) for k in range(2)]
         for tile in f1:
             nc.vector.memset(tile[:], 0.0)
-        for tile in f2:
-            nc.gpsimd.memset(tile[:], 0.0)
 
+        load_plane(nc.scalar, keys_plane, keys_scales)
         query_raw = [load_query(query, "query_raw0", 0, Q // 2)]
-        load_plane(keys_plane, keys_scales)
         query_raw.append(load_query(query, "query_raw1", Q // 2, Q))
         keys_codes = keep.tile([P, 2 * T], U8, name="keys_codes", align_bytes=64)
         nc.sync.dma_start(out=keys_codes[:].bitcast(I32), in_=keys_words[0].bitcast(I32))
@@ -99,7 +95,7 @@ def tile_attend_returned_twoq_mixed_kernel(tc, query, query2, keys_words, keys_s
         notes_codes = keep.tile([P, U], U32, name="notes_codes", align_bytes=64)
         nc.sync.dma_start(out=notes_codes[:].bitcast(I32),
                           in_=notes_words[0].rearrange("p n r -> p (n r)").bitcast(I32))
-        load_plane(notes_plane, notes_scales)
+        load_plane(nc.sync, notes_plane, notes_scales)
         list3 = load_list(offs3, "list3")
         list4 = load_list(offs4, "list4")
         list5 = load_list(offs5, "list5")
@@ -109,7 +105,7 @@ def tile_attend_returned_twoq_mixed_kernel(tc, query, query2, keys_words, keys_s
         mix_codes = keep.tile([P, E], U32, name="mix_codes", align_bytes=64)
         nc.sync.dma_start(out=mix_codes[:].bitcast(I32),
                           in_=mix_words[0].rearrange("p n r -> p (n r)").bitcast(I32))
-        load_plane(mix_plane, mix_scales)
+        load_plane(nc.sync, mix_plane, mix_scales)
 
         def keys_moving(cols):
             return keys_codes[:, 2 * cols.start:2 * cols.stop].bitcast(FP4X4)
@@ -141,18 +137,20 @@ def tile_attend_returned_twoq_mixed_kernel(tc, query, query2, keys_words, keys_s
                     else:
                         gather(a_half[:], a[t], list1[:, list_halves[h]])
                     nc.vector.tensor_copy(f1[0][:].indirect(list2[:, list_halves[h]]), a_half[:])
-                dealt2 = keep.tile([P, PACK, P, PACK], BF16, name="dealt2", tag="dealt2", align_bytes=64)
-                deal(gpsimd_round, dealt2, query2_raw, slice(0, P), slice(0, PACK), "p t m j")
-                rows2 = quantize_tiles(dealt2, 0, PACK, "q2all")
-                f1.append(keep.tile([P, U], F32, name="f1_3", tag="dealt2", align_bytes=64))
-                nc.gpsimd.memset(f1[PACK - 1][:], 0.0)
             else:
-                a_picked = ring.tile([P, I], F32, name="a_picked")
+                a_picked = keep.tile([P, I], F32, name="a_picked%d" % t, tag="a_picked%d" % t, align_bytes=64)
                 gather(a_picked[:], a[t], list1[:])
                 if t == PACK - 1:
-                    f1_picked.append(keep.tile([P, I], F32, name="f1_picked0"))
+                    f1_picked.append(keep.tile([P, I], F32, name="f1_picked0", tag="f1_picked0"))
                     gather(f1_picked[0][:], f1[0], list3[:])
                 nc.vector.tensor_copy(f1[t][:].indirect(list2[:]), a_picked[:])
+            if t == 1:
+                for k in range(PACK):
+                    dealt2 = keep.tile([P, 1, P, PACK], BF16, name="dealt2_%d" % k, tag="dealt2_%d" % k, align_bytes=64)
+                    gpsimd_round(dealt2[:, 0], query2_raw[:].rearrange("p j (m t) -> p t m j", t=PACK)[:, k])
+                    rows2 = rows2 + quantize_tiles(dealt2, 0, 1, "q2_%d" % k, "a_picked1" if k == 0 else None)
+                f1.append(keep.tile([P, U], F32, name="f1_3", tag="dealt2_0", align_bytes=64))
+                nc.gpsimd.memset(f1[PACK - 1][:], 0.0)
 
         b_picked = []
         for t in range(PACK):
@@ -171,7 +169,11 @@ def tile_attend_returned_twoq_mixed_kernel(tc, query, query2, keys_words, keys_s
             nc.vector.tensor_tensor(w[:], f1_picked[t][:], b_picked[t][:], ALU.max)
             return w
 
+        f2 = [keep.tile([P, T], F32, name="f2_0", tag="a_picked2", align_bytes=64)]
+        nc.gpsimd.memset(f2[0][:], 0.0)
         w = larger(0)
+        f2.append(keep.tile([P, T], F32, name="f2_1", tag="f1_picked0"))
+        nc.gpsimd.memset(f2[1][:], 0.0)
         for t in range(PACK):
             nc.vector.tensor_copy(f2[t % 2][:].indirect(list5[:]), w[:])
             last = t == PACK - 1

@@ -49,9 +49,9 @@ def tile_attend_returned_twoq_mixed_kernel(tc, query, query2, keys_words, keys_s
             nc.sync.dma_start(out=raw[:], in_=source.rearrange("(p j) q -> p j q", j=PACK)[:, :, first:end])
             return raw
 
-        def deal(cast, dealt, raw, rows, tiles, walk):
-            cast(out=dealt[:, tiles, rows, :].rearrange("p t m j -> " + walk),
-                 in_=raw[:].rearrange("p j (m t) -> p t m j", t=PACK)[:, tiles].rearrange("p t m j -> " + walk))
+        def deal(cast, dealt, raws, h, tiles):
+            cast(out=dealt[:, tiles, h * (P // 2):(h + 1) * (P // 2), :],
+                 in_=raws[h][:].rearrange("p j (m t) -> p t m j", t=PACK)[:, tiles])
 
         def gpsimd_round(out, in_):
             nc.gpsimd.tensor_scalar(out, in_, 1.0, 0.0, ALU.mult, ALU.add)
@@ -117,10 +117,12 @@ def tile_attend_returned_twoq_mixed_kernel(tc, query, query2, keys_words, keys_s
         in_turn = (nc.scalar.copy, nc.vector.tensor_copy) * 2
 
         dealt = keep.tile([P, PACK, P, PACK], BF16, name="dealt", align_bytes=64)
-        deal(nc.vector.tensor_copy, dealt, query_raw[0], slice(0, P // 2), slice(0, PACK), "p m j t")
-        deal(nc.vector.tensor_copy, dealt, query_raw[1], slice(P // 2, P), slice(0, 1), "p m j t")
+        deal(nc.vector.tensor_copy, dealt, query_raw, 0, slice(0, 2))
+        deal(nc.scalar.copy, dealt, query_raw, 0, slice(2, PACK))
+        deal(nc.vector.tensor_copy, dealt, query_raw, 1, slice(0, 1))
         rows = quantize_tiles(dealt, 0, 1, "q0")
-        deal(nc.vector.tensor_copy, dealt, query_raw[1], slice(P // 2, P), slice(1, PACK), "p m j t")
+        deal(nc.vector.tensor_copy, dealt, query_raw, 1, slice(1, 2))
+        deal(nc.scalar.copy, dealt, query_raw, 1, slice(2, PACK))
         rows = rows + quantize_tiles(dealt, 1, 1, "q1") + quantize_tiles(dealt, 2, 2, "q2")
 
         halves = [slice(h * HALF, (h + 1) * HALF) for h in range(2)]

from contextlib import ExitStack

import concourse.mybir as mybir

D, T, U, I, Q, E = 512, 1024, 1024, 512, 512, 256
FLOPS = 2 * D * Q * T + 2 * D * Q * U + 2 * Q * E * I

F32 = mybir.dt.float32
BF16 = mybir.dt.bfloat16
I32 = mybir.dt.int32
U32 = mybir.dt.uint32
U16 = mybir.dt.uint16
U8 = mybir.dt.uint8
FP8X4 = mybir.dt.float8_e4m3fn_x4
FP4X4 = mybir.dt.float4_e2m1fn_x4
COPY = mybir.ActivationFunctionType.Copy
ALU = mybir.AluOpType

P = 128
PACK = 4
BANK = 512
HALF = I // 2


def tile_attend_returned_twoq_mixed_kernel(tc, query, query2, keys_words, keys_scales, notes_words, notes_scales,
                                            rowf, mix_words, mix_scales, offs, offs2, offs3, offs4, offs5, offs6, out):
    nc = tc.nc
    with ExitStack() as ctx:
        keep = ctx.enter_context(tc.tile_pool(name="keep", bufs=1))
        ring = ctx.enter_context(tc.tile_pool(name="ring", bufs=2))
        score_banks = ctx.enter_context(tc.psum_pool(name="score_banks", bufs=8))

        def load_list(source, name):
            tile = keep.tile([P, I // 16], U16, name=name)
            nc.sync.dma_start(tile[:], source)
            return tile

        def scale_plane(width, name):
            plane = keep.tile([P, width], U8, name=name, align_bytes=64)
            return plane

        def load_plane(queue, plane, scales):
            for quad in range(4):
                queue.dma_start(out=plane[32 * quad:32 * quad + 4, :].bitcast(I32),
                                in_=scales[0, 4 * quad:4 * quad + 4, :].bitcast(I32))

        def load_query(source, name, first, end):
            raw = keep.tile([P, PACK, end - first], F32, name=name)
            nc.sync.dma_start(out=raw[:], in_=source.rearrange("(p j) q -> p j q", j=PACK)[:, :, first:end])
            return raw

        def deal(cast, dealt, raws, h, tiles):
            cast(out=dealt[:, tiles, h * (P // 2):(h + 1) * (P // 2), :],
                 in_=raws[h][:].rearrange("p j (m t) -> p t m j", t=PACK)[:, tiles])

        def gpsimd_round(out, in_):
            nc.gpsimd.tensor_scalar(out, in_, 1.0, 0.0, ALU.mult, ALU.add)

        def quantize_tiles(dealt, first, count, name, tag=None):
            codes = keep.tile([P, count * P], U32, name=name + "_codes", tag=tag or name + "_codes", align_bytes=64)
            scales = keep.tile([P, count * P], U8, name=name + "_scales", align_bytes=64)
            nc.vector.quantize_mx(out=codes[:].bitcast(FP8X4), scales=scales[:],
                                  in_=dealt[:, first:first + count].rearrange("p t m j -> p (t m j)"))
            return [(codes[:, k * P:(k + 1) * P].bitcast(FP8X4), scales[:, k * P:(k + 1) * P]) for k in range(count)]

        def score(rows, moving, plane, name, engines):
            scores = keep.tile([P, T], F32, name=name, tag=name)
            width = T // len(engines)
            for n, copy_out in enumerate(engines):
                cols = slice(n * width, (n + 1) * width)
                bank = score_banks.tile([P, BANK], F32, name="bank")
                nc.tensor.matmul_mx(out=bank[:, :width], lhsT=rows[0], lhsT_scale=rows[1], rhs=moving(cols),
                                    rhs_scale=plane[:, cols], start=True, stop=True)
                copy_out(out=scores[:, cols], in_=bank[:, :width])
            return scores

        def gather(picked, window, offsets):
            nc.scalar.activation(picked, window[:].indirect(offsets), COPY)

        keys_plane = scale_plane(T, "keys_plane")
        notes_plane = scale_plane(U, "notes_plane")
        mix_plane = scale_plane(E, "mix_plane")
        f1 = [keep.tile([P, U], F32, name="f1_%d" % k) for k in range(PACK - 1)]
        for tile in f1:
            nc.vector.memset(tile[:], 0.0)

        load_plane(nc.scalar, keys_plane, keys_scales)
        query_raw = [load_query(query, "query_raw0", 0, Q // 2)]
        query_raw.append(load_query(query, "query_raw1", Q // 2, Q))
        keys_codes = keep.tile([P, 2 * T], U8, name="keys_codes", align_bytes=64)
        nc.sync.dma_start(out=keys_codes[:].bitcast(I32), in_=keys_words[0].bitcast(I32))
        list1 = load_list(offs, "list1")
        list2 = load_list(offs2, "list2")
        query2_raw = load_query(query2, "query2_raw", 0, Q)
        notes_codes = keep.tile([P, U], U32, name="notes_codes", align_bytes=64)
        nc.sync.dma_start(out=notes_codes[:].bitcast(I32),
                          in_=notes_words[0].rearrange("p n r -> p (n r)").bitcast(I32))
        load_plane(nc.sync, notes_plane, notes_scales)
        list3 = load_list(offs3, "list3")
        list4 = load_list(offs4, "list4")
        list5 = load_list(offs5, "list5")
        list6 = load_list(offs6, "list6")
        factors = keep.tile([P, PACK], F32, name="factors")
        nc.sync.dma_start(out=factors[:], in_=rowf.rearrange("(p t) o -> p (t o)", t=PACK))
        mix_codes = keep.tile([P, E], U32, name="mix_codes", align_bytes=64)
        nc.sync.dma_start(out=mix_codes[:].bitcast(I32),
                          in_=mix_words[0].rearrange("p n r -> p (n r)").bitcast(I32))
        load_plane(nc.sync, mix_plane, mix_scales)

        def keys_moving(cols):
            return keys_codes[:, 2 * cols.start:2 * cols.stop].bitcast(FP4X4)

        def notes_moving(cols):
            return notes_codes[:, cols].bitcast(FP8X4)

        both_scalar = (nc.scalar.copy, nc.scalar.copy)
        in_turn = (nc.scalar.copy, nc.vector.tensor_copy) * 2

        dealt = keep.tile([P, PACK, P, PACK], BF16, name="dealt", align_bytes=64)
        deal(nc.vector.tensor_copy, dealt, query_raw, 0, slice(0, 2))
        deal(nc.scalar.copy, dealt, query_raw, 0, slice(2, PACK))
        deal(nc.vector.tensor_copy, dealt, query_raw, 1, slice(0, 1))
        rows = quantize_tiles(dealt, 0, 1, "q0")
        deal(nc.vector.tensor_copy, dealt, query_raw, 1, slice(1, 2))
        deal(nc.scalar.copy, dealt, query_raw, 1, slice(2, PACK))
        rows = rows + quantize_tiles(dealt, 1, 1, "q1") + quantize_tiles(dealt, 2, 2, "q2")

        halves = [slice(h * HALF, (h + 1) * HALF) for h in range(2)]
        list_halves = [slice(h * HALF // 16, (h + 1) * HALF // 16) for h in range(2)]

        a, rows2, f1_picked = [], [], []
        for t in range(PACK):
            a.append(score(rows[t], keys_moving, keys_plane, "a%d" % t, in_turn if t == 0 else both_scalar))
            if t == 0:
                for h in range(2):
                    a_half = keep.tile([P, HALF], F32, name="a_half%d" % h)
                    if h == 0:
                        nc.vector.tensor_copy(a_half[:], a[t][:].indirect(list1[:, list_halves[h]]))
                    else:
                        gather(a_half[:], a[t], list1[:, list_halves[h]])
                    nc.vector.tensor_copy(f1[0][:].indirect(list2[:, list_halves[h]]), a_half[:])
            else:
                a_picked = keep.tile([P, I], F32, name="a_picked%d" % t, tag="a_picked%d" % t, align_bytes=64)
                gather(a_picked[:], a[t], list1[:])
                if t == PACK - 1:
                    f1_picked.append(keep.tile([P, I], F32, name="f1_picked0", tag="f1_picked0"))
                    gather(f1_picked[0][:], f1[0], list3[:])
                nc.vector.tensor_copy(f1[t][:].indirect(list2[:]), a_picked[:])
            if t == 1:
                for k in range(PACK):
                    dealt2 = keep.tile([P, 1, P, PACK], BF16, name="dealt2_%d" % k, tag="dealt2_%d" % k, align_bytes=64)
                    gpsimd_round(dealt2[:, 0], query2_raw[:].rearrange("p j (m t) -> p t m j", t=PACK)[:, k])
                    rows2 = rows2 + quantize_tiles(dealt2, 0, 1, "q2_%d" % k, "a_picked1" if k == 0 else None)
                f1.append(keep.tile([P, U], F32, name="f1_3", tag="dealt2_0", align_bytes=64))
                nc.gpsimd.memset(f1[PACK - 1][:], 0.0)

        b_picked = []
        for t in range(PACK):
            if t > 0:
                f1_picked.append(keep.tile([P, I], F32, name="f1_picked%d" % t, tag="b%d" % (t - 1)))
                gather(f1_picked[t][:], f1[t], list3[:])
            b = score(rows2[t], notes_moving, notes_plane, "b%d" % t, both_scalar)
            b_picked.append(keep.tile([P, I], F32, name="b_picked%d" % t))
            gather(b_picked[t][:], b, list4[:])

        gw = keep.tile([P, I, PACK], BF16, name="gw", align_bytes=64)
        g_last = []

        def larger(t):
            w = ring.tile([P, I], F32, name="w")
            nc.vector.tensor_tensor(w[:], f1_picked[t][:], b_picked[t][:], ALU.max)
            return w

        f2 = [keep.tile([P, T], F32, name="f2_0", tag="a_picked2", align_bytes=64)]
        nc.gpsimd.memset(f2[0][:], 0.0)
        w = larger(0)
        f2.append(keep.tile([P, T], F32, name="f2_1", tag="f1_picked0"))
        nc.gpsimd.memset(f2[1][:], 0.0)
        for t in range(PACK):
            nc.vector.tensor_copy(f2[t % 2][:].indirect(list5[:]), w[:])
            last = t == PACK - 1
            if not last:
                w = larger(t + 1)
            cc = keep.tile([P, T], F32, name="cc%d" % t, tag="cc3" if last else "b%d" % t)
            add = nc.vector.tensor_tensor if last else nc.gpsimd.tensor_tensor
            add(cc[:], a[t][:], f2[t % 2][:], ALU.add)
            g = keep.tile([P, I], F32, name="g%d" % t, tag="b3" if t == 0 else "g%d" % t)
            if not last:
                gather(g[:], cc, list6[:])
                if t < 2:
                    nc.scalar.activation(gw[:, :, t], g[:], COPY, scale=factors[:, t:t + 1])
                else:
                    nc.vector.tensor_scalar(gw[:, :, t], g[:], factors[:, t:t + 1], None, ALU.mult)
            else:
                for h in range(2):
                    gather(g[:, halves[h]], cc, list6[:, list_halves[h]])
                    g_last.append(g[:, halves[h]])

        for h in range(2):
            slots = halves[h]
            nc.vector.tensor_scalar(gw[:, slots, PACK - 1], g_last[h], factors[:, PACK - 1:PACK], None, ALU.mult)
            gw_codes = keep.tile([P, HALF], U32, name="gw_codes%d" % h, align_bytes=64)
            gw_scales = keep.tile([P, HALF], U8, name="gw_scales%d" % h, align_bytes=64)
            nc.vector.quantize_mx(out=gw_codes[:].bitcast(FP8X4), scales=gw_scales[:],
                                  in_=gw[:, slots, :].rearrange("p i t -> p (i t)"))
            for c in range(E // P):
                bank = score_banks.tile([P, BANK], F32, name="bank")
                nc.tensor.matmul_mx(out=bank[:, :HALF], lhsT=mix_codes[:, c * P:(c + 1) * P].bitcast(FP8X4),
                                    lhsT_scale=mix_plane[:, c * P:(c + 1) * P], rhs=gw_codes[:].bitcast(FP8X4),
                                    rhs_scale=gw_scales[:], start=True, stop=True)
                result = keep.tile([P, HALF], F32, name="result%d_%d" % (h, c))
                copy_out = nc.vector.tensor_copy if (h, c) == (1, 1) else nc.scalar.copy
                copy_out(out=result[:], in_=bank[:, :HALF])
                nc.sync.dma_start(out=out[c * P:(c + 1) * P, slots], in_=result[:])
